import numpy as np, ml_dtypes
CORES = [113,118,241,246]
N = 4
BF = ml_dtypes.bfloat16
def gentries(a):
    return np.ascontiguousarray(a.reshape(8, 16, -1).transpose(0, 2, 1)).reshape(8, -1)
def gtable(e):
    e = np.asarray(e); return np.ascontiguousarray(e.reshape(8, -1, 16).transpose(0, 2, 1)).reshape(128, -1).astype(np.int32)
W, T, L, RO = 1536, 512, 4, 3
R = W >> 7
def chain(par, a):
    c = [a]
    for i in range(L - 1): c.append(np.take_along_axis(par, c[-1], 1))
    return np.stack(c, axis=1)
def meeting(ca, cb):
    eq = (ca[:, :, None] == cb[:, None]).reshape(8, L * L, T)
    found = np.any(eq, axis=1); first = np.argmax(eq, axis=1); i = first // L
    return found, np.where(found, i, 0), np.where(found, first - L * i, 0)
def one_round(f, par, a, b, own):
    ca, cb = chain(par, a), chain(par, b); found, I, J = meeting(ca, cb)
    pos = np.arange(L)[None, :, None]
    both = np.concatenate([ca, cb], axis=1); on = np.concatenate([pos < I[:, None], pos < J[:, None]], axis=1)
    mine = np.take_along_axis(own, both.reshape(8, -1), 1).reshape(8, 2 * L, T) == np.arange(T)
    kept = np.all(mine | ~on, axis=1)
    v = np.take_along_axis(f, both.reshape(1, 8, 1, -1), 3).reshape(N, 8, 16, 2 * L, T)
    sg = np.repeat(np.array([1, -1]), L)[:, None]
    D = np.sum(v * (sg * on)[None, :, None], axis=3, keepdims=True)
    n = (I + J + 1)[None, :, None, None]
    votes = np.sum((n * v <= sg * D) & on[None, :, None], axis=(0, 2))
    place = np.where(votes > 8 * N, np.tile(np.arange(L), 2)[:, None], -1)
    ka, kb = np.max(place[:, :L], axis=1), np.max(place[:, L:], axis=1)
    side = ka < 0; k = np.where(side, kb, ka); go = kept & found & (k >= 0); k = np.maximum(k, 0)
    s3 = side[:, None]; s5 = side[None, :, None, None]
    P, Q = np.where(s3, cb, ca), np.where(s3, ca, cb); X, Y = np.where(side, J, I), np.where(side, I, J)
    vp, vq = np.where(s5, v[:, :, :, L:], v[:, :, :, :L]), np.where(s5, v[:, :, :, :L], v[:, :, :, L:])
    M = np.take_along_axis(vp, k[None, :, None, None], 3)
    before = np.concatenate([np.zeros_like(M), vp[:, :, :, :-1]], axis=3)
    turn = pos <= k[:, None]
    newp = np.where(turn[None, :, None], M - before, vp - M); newq = vq + M
    g3 = go[:, None]
    to = np.concatenate([np.where(g3 & (pos < X[:, None]), P, W), np.where(g3 & (pos < Y[:, None]), Q, W)], axis=1)
    f2 = np.concatenate([f, np.zeros((N, 8, 16, 1), f.dtype)], axis=3)
    np.put_along_axis(f2, to.reshape(1, 8, 1, -1), np.concatenate([newp, newq], axis=3).reshape(N, 8, 16, -1), 3)
    p2 = np.concatenate([par, np.zeros((8, 1), par.dtype)], axis=1)
    np.put_along_axis(p2, np.where(g3 & turn, P, W).reshape(8, -1), np.concatenate([Q[:, :1], P[:, :-1]], axis=1).reshape(8, -1), 1)
    na = np.where(go, np.take_along_axis(P, k[:, None], 1)[:, 0], a)
    nb = np.where(go, np.take_along_axis(P, np.minimum(k + 1, L - 1)[:, None], 1)[:, 0], b)
    return f2[..., :W], p2[:, :W], na, nb
def forest(rng, q, ends):
    x = np.arange(W)
    pp = np.where(rng.random((8, W)) < q, x - R, x - 1 - (rng.random((8, W)) * np.minimum(x, 3 * R)).astype(np.int64)); pp[:, :R] = x[:R]
    lab = np.argsort(rng.random((8, W)), axis=1)
    if ends:
        for g in range(8):
            for at, num in ((W - 1, 0), (0, W - 1)):
                j = int(np.argmax(lab[g] == num)); lab[g, j] = lab[g, at]; lab[g, at] = num
    return pp, lab
def flows(rng, pp, lab):
    base = np.where(rng.random((W, 8, 1, 1)) < 0.55, np.exp2(6 * rng.random((W, 8, 1, 1))), 0)
    c = (2 * base * rng.random((W, 8, N, 16))).astype(np.int64); ar = np.arange(8)
    for x in range(W - 1, R - 1, -1): c[pp[:, x], ar] += c[x]
    f = np.zeros((N, 8, 16, W), np.int64)
    np.put_along_axis(f, lab[None, :, None], np.minimum(c, 4095).transpose(2, 1, 3, 0), 3)
    return f
def lay(rng, p, lo, spoil, fix=(), hold=()):
    kids = [[] for v in range(W)]
    for v in range(W):
        if p[v] != v: kids[p[v]].append(v)
    leaf = np.array([not c for c in kids])
    o = np.argsort(rng.random(W) + np.where(~leaf & (rng.random(W) < 0.7), 1.0, 0.0)); o = np.concatenate([np.array([0, W - 1]), o[(o != 0) & (o != W - 1)]])
    wi = np.where(rng.random(W) < 0.06, L, rng.integers(lo, L, W)); wj = np.where(rng.random(W) < 0.06, L, rng.integers(lo - 1, L, W))
    num = rng.permutation(T).tolist(); own = rng.integers(0, T, W).tolist(); a, b = rng.integers(0, W, (2, T)); free = [True] * W; made = 0
    for y in hold: free[y] = False
    tops = [v for v in range(W) if p[v] == v]; tops = [tops[i] for i in rng.permutation(len(tops))]; low = []
    for v in tops[:2 * (len(tops) // 4)]:
        for s in range(int(rng.integers(0, L))):
            if kids[v]: v = kids[v][int(rng.integers(0, len(kids[v])))]
        low.append(v)
    pairs = [(u, v) for u, v in fix] + [(u, v) for u, v in zip(low[::2], low[1::2])]
    for u, v in pairs:
        cu, cv = [u], [v]
        for s in range(L - 1):
            cu.append(p[cu[-1]]); cv.append(p[cv[-1]])
        i = next((s for s in range(L) if cu[s] in cv), L); j = cv.index(cu[i]) if i < L else L
        z = num[made]; made += 1; a[z] = u; b[z] = v
        for y in cu[:i] + cv[:j]:
            free[y] = False; own[y] = z
    for v, i, j in zip(o.tolist(), wi.tolist(), wj.tolist()):
        if made >= 15 * T // 16: break
        if not free[v] or p[v] == v: continue
        up = [v]; dn = []; x = p[v]
        while len(up) < i and free[x] and p[x] != x:
            up.append(x); x = p[x]
        while len(dn) < j:
            c = [y for y in kids[x] if free[y] and y != up[-1]]
            if not c: break
            c = [y for y in c if kids[y]] or c
            x = c[made % len(c)]; dn.append(x)
        z = num[made]; made += 1; a[z] = v; b[z] = x
        for y in up + dn:
            free[y] = False; own[y] = z
        if spoil > 0 and rng.random() < (0.5 if z >= T - 2 else spoil):
            near = z >= T - 2 or rng.random() < 0.5
            own[(up + dn)[int(rng.integers(0, len(up) + len(dn)))]] = z ^ 1 if near else (z + 1 + int(rng.integers(0, T - 1))) % T
    for i, z in enumerate(num[made:]):
        x = int(a[z])
        if i % 4 == 0: b[z] = x
        if i % 4 == 1:
            for s in range(1 + (i >> 2) % L): x = p[x]
            b[z] = x
        if i % 4 == 2:
            c = kids[p[p[x]]]
            if c: b[z] = c[i % len(c)]
    sw = rng.random(T) < 0.5; sw[np.array(num[:len(pairs)], np.int64)] = False
    return np.where(sw, b, a), np.where(sw, a, b), np.array(own)
def numbered(rng, up, fp, fix, hold):
    lab = rng.permutation(W); par = np.zeros(W, np.int64); par[lab] = lab[np.array(up)]
    f = np.zeros((N, 16, W), np.int64); f[:, :, lab] = fp
    return par, f, [[(int(lab[u]), int(lab[v])) for u, v in x] for x in fix], [int(lab[y]) for y in hold]
def beads(rng, line=False):
    most = L - 1 if line else 2 * (L - 1); total = min(W - 1, most * T); n = total // T + (np.arange(T) < total % T).astype(np.int64)
    o = rng.permutation(T); x, y = o[:T // 2], o[T // 2:]
    d = (rng.random(T // 2) * (np.minimum(most - n[x], n[y] - 1) + 1)).astype(np.int64); n[x] += d; n[y] -= d
    gap = np.bincount(rng.integers(0, T, W - 1 - total), minlength=T).tolist(); n = n.tolist()
    fp = rng.integers(0, 4096, (N, 16, W)); up = [0]; x = 0; fix = []
    for j in range(T):
        i = n[j] if line else int(rng.integers(max(0, n[j] - L + 1), min(n[j], L - 1) + 1)); br = []
        for c in (i, n[j] - i):
            y = x; z = []
            for s in range(c):
                up.append(y); y = len(up) - 1; z.append(y)
            br.append(z)
        A, B = br; fix.append((A[-1] if A else x, B[-1] if B else x))
        P, Q = (A, B) if len(A) >= len(B) else (B, A)
        fp[:, :, P] = rng.integers(2048, 4096, (N, 16, len(P)))
        if Q: fp[:, :, Q] = rng.integers(0, min(4095, 2048 * (len(P) - 1) // len(Q)) + 1, (N, 16, len(Q)))
        who = (rng.permutation(16 * N) < int(rng.integers(8 * N + 1, 16 * N + 1))).reshape(N, 16)
        m = P[int(rng.integers(0, len(P)))]; fp[:, :, m] = np.where(who, 0, fp[:, :, m]); x = P[-1]
        for s in range(gap[j]):
            up.append(x); x = len(up) - 1
    return numbered(rng, up, fp, [fix] + [[] for t in range(RO - 1)], [])
def straight(rng):
    return beads(rng, True)
def heavy(rng):
    S = L - 1; top = ((L - 2) * 4000 - 4095) // L; light = ((L - 2) * 4095 // S + (L - 2) * (top + 3995) // S) // 2
    up = [0]; fp = rng.integers(0, 4096, (N, 16, W)); fix = [[] for t in range(RO)]
    def put(at, lo, hi):
        up.append(at); fp[:, :, len(up) - 1] = rng.integers(lo, hi + 1, (N, 16))
        return len(up) - 1
    def lift(at, m, weak):
        q = put(at, light - 520, light - 480) if weak else put(at, 4045, 4095); y = at; P = []
        for s in range(S - 1, -1, -1):
            y = put(y, 4000, 4095) if s != m else put(y, 500, 500) if weak else put(y, top - 50, top)
            P.append(y)
        fix[0].append((y, q))
        return q, P[::-1]
    x = 0
    for u in range(16):
        x = put(x, 0, 4095); y1 = put(x, 0, 0); y0 = put(y1, 4000, 4095); fix[0].append((y0, x))
        weak = int(rng.integers(0, S)); y = x
        for i in range(S): y = lift(y, int(rng.integers(0, S)), u % 2 == 1 and i == weak)[0]
        fix[1].append((y, x if u % 2 == 1 else y1))
    if RO > 2:
        for u in range(8):
            x = put(x, 0, 4095); y1 = put(x, 0, 0); y0 = put(y1, 4000, 4095); fix[0].append((y0, x))
            q, P = lift(y0, 1, False); q2 = lift(y1, int(rng.integers(0, S)), False)[0]; q1 = lift(q2, int(rng.integers(0, S)), False)[0]
            fix[1].append((P[1], y0)); fix[1].append((q1, y0)); fix[2].append((P[0], y1))
    hold = [y for y in range(len(up))]
    while len(up) < W: up.append(len(up) - 1 - int(rng.random() * min(len(up), 3 * R)))
    return numbered(rng, up, fp, fix, hold)
def draw(rng, q=0.7, lo=1, spoil=0.12, ends=False, change=None, plant=None, still=False, make=()):
    pp, lab = forest(rng, q, ends); par = np.zeros((8, W), np.int64); np.put_along_axis(par, lab, np.take_along_axis(lab, pp, 1), 1)
    f = flows(rng, pp, lab) if change is None else change(rng)
    ts = []; rs = []; quiet = rng.permutation(8).tolist(); one = int(rng.integers(0, T))
    fix = [[[] for t in range(RO)] for g in range(8)]; hold = [[] for g in range(8)]
    for g, m in zip(quiet[2:], make):
        par[g], f[:, g], fix[g], hold[g] = m(rng)
    now = par
    for t in range(RO):
        z = [lay(rng, now[g].tolist(), lo, spoil, fix[g][t], hold[g]) for g in range(8)]
        a, b, own = [np.stack([y[i] for y in z]) for i in range(3)]
        if still:
            b[quiet[0]] = a[quiet[0]]; own[quiet[1]] = one
        if t == 0:
            if plant is not None: f = plant(rng, f, now, a, b, own)
            f0 = f
        ts.append(np.concatenate([a, b], axis=1)); rs.append(own)
        if t < RO - 1: f, now, a, b = one_round(f, now, a, b, own)
    return {"fl": np.ascontiguousarray(f0.reshape(N, 128, W)).astype(np.float32), "par": np.stack([par] * N).astype(np.int32),
            "tie": np.stack([gtable(np.concatenate(ts, axis=1))] * N), "res": np.stack([np.concatenate(rs, axis=1)] * N).astype(np.int32)}
def exact_votes(rng, f, par, a, b, own):
    f = f.copy(); ca, cb = chain(par, a), chain(par, b); found, I, J = meeting(ca, cb)
    for g in range(8):
        for j in range(T):
            X, Y = int(I[g, j]), int(J[g, j]); P, Q = ca[g, :X, j], cb[g, :Y, j]
            if X + Y == 0 or np.any(own[g, P] != j) or np.any(own[g, Q] != j): continue
            if X == 0 or (Y > 0 and rng.random() < 0.5): X, Y, P, Q = Y, X, Q, P
            m = int(rng.integers(0, X)); z = int(m > 0 and rng.random() < 0.5)
            h = int(rng.integers(1, 4095 // (X + Y) + 1)); top = (X - 1 - z) * h
            c = (8 * N - 1, 8 * N, 8 * N + 1, 8 * N + 2, 0, 16 * N)[(g + j) % 6]
            who = (rng.permutation(16 * N) < c).reshape(N, 16)
            if rng.random() < 0.5: who = rng.permuted((np.arange(16 * N) < c).reshape(N, 16)[rng.permutation(N)], axis=1)
            less = top - rng.integers(0, top + 1, (N, 16)) * rng.integers(0, 2, (N, 16))
            f[:, g, :, P] = (X + Y) * h; f[:, g, :, Q] = 0
            if z: f[:, g, :, int(P[m - 1])] = 0
            f[:, g, :, int(P[m])] = np.where(who, less, top + 1)
    return f
def few(rng):
    vals = np.array([0, 0, 0, 1, 2, 4095]); k = rng.choice(vals, (1, 8, 1, W))
    return np.where(rng.random((N, 8, 16, W)) < 0.15, rng.choice(vals, (N, 8, 16, W)), k)
def uneven(rng):
    return np.minimum((np.exp2(12 * rng.random((1, 8, 1, W))) * rng.random((N, 8, 16, W))).astype(np.int64), 4095)
def setup_inputs(rng):
    return draw(rng)
def setup_inputs_votes(rng):
    return draw(rng, spoil=0.05, plant=exact_votes)
def setup_inputs_ends(rng):
    return draw(rng, q=0.85, lo=L - 1, ends=True, make=(straight, beads))
def setup_inputs_flat(rng):
    return draw(rng, change=few, make=(heavy,))
def setup_inputs_still(rng):
    return draw(rng, q=0.6, spoil=0.0, still=True)
def setup_inputs_spread(rng):
    return draw(rng, q=0.75, change=uneven)
def check_inputs(d):
    bad = []
    for k, lo, hi in (("fl", 0, 4095), ("par", 0, W - 1), ("tie", 0, W - 1), ("res", 0, T - 1)):
        if not (np.min(d[k]) >= lo and np.max(d[k]) <= hi): bad.append("range of " + k)
    if np.any(d["fl"] != np.floor(d["fl"])): bad.append("whole numbers in fl")
    for k in ("par", "tie", "res"):
        if np.any(d[k] != d[k][:1]): bad.append(k + " alike on all ranks")
    if "range of par" not in bad:
        p = d["par"].astype(np.int64).reshape(-1, W); q = p
        for i in range(12): q = np.take_along_axis(q, q, 1)
        if np.any(np.take_along_axis(p, q, 1) != q): bad.append("every bus has a root")
    return bad
def reference(fl, par, tie, res):
    f = fl.astype(np.int64).reshape(N, 8, 16, W); p = par[0].astype(np.int64)
    e = gentries(tie[0]).astype(np.int64).reshape(8, RO, 2, T); own = res[0].astype(np.int64).reshape(8, RO, W); new = np.zeros_like(e)
    for t in range(RO):
        f, p, na, nb = one_round(f, p, e[:, t, 0], e[:, t, 1], own[:, t])
        new[:, t, 0] = na; new[:, t, 1] = nb
    return {"yf": f.reshape(N, 128, W).astype(np.float32), "yp": np.stack([p] * N).astype(np.float32), "yt": np.stack([gtable(new.reshape(8, -1))] * N).astype(np.float32)}

from concourse.bass import DstId, RemoteDMATransfer
from concourse.mybir import AluOpType as A, ActivationFunctionType as AF

NB, NT, RO = 1536, 512, 3
W1, W2 = 64, 3968
EPS = 1.0 / 16
CODE = ((5, 1), (6, 2), (7, 3))
TS, TL = 48, 36
OLD = [(0, 0), (0, 1), (1, 0), (1, 1), (2, 0), (2, 1), (2, 2), (0, 2), (1, 2)]
PAIRS = OLD + [(0, 3), (3, 0), (1, 3), (3, 1), (2, 3), (3, 2), (3, 3)]

f32, b16, h16, i32, u16 = "float32", "bfloat16", "float16", "int32", "uint16"
_SB = {
    "W": (7176, f32), "PW": (7168, b16), "votes": (3072, b16), "iov": (NB, f32), "base": (NB, f32), "oh": (NB, b16),
    "eg": (NB, b16), "O": (3072, b16), "Lb": (2048, b16), "Lf": (2048, f32), "Zi": (16 * 144, h16), "Z": (11 * 144, b16),
    "Sel": (9 * 128, b16), "Ih": (256, h16), "cols": (144, f32), "pi": (8, i32), "cf": (16, f32), "hv": (8, f32),
    "ev": (32, f32), "bb": (384, f32), "Xi": (480, i32), "XH": (480, b16), "XL": (480, b16), "tiei": (192, i32), "tieu": (192, u16),
    "vl": (96, f32), "zh": (64, h16), "wt": (192, f32), "Cu": (128, u16), "Ch": (256, h16), "E": (512, b16), "ones": (32, b16),
    "SLu": (192, u16), "SLh": (192, h16), "on": (192, b16), "m": (192, b16), "mis": (192, b16), "nf": (32, b16),
    "rn": (32, f32), "Dsb": (NT, f32), "Dp": (NT, f32), "slotw": (NT, f32), "dwin": (NT, b16), "ytg": (NT, b16), "yts": (192, f32),
    "yps": (NB, f32), "ru": (288, u16), "zc": (288, f32), "zv": (192, f32),
    "snd": (192, u16), "land": (576, u16), "lf": (192, f32), "s1": (64, f32), "S": (64, i32), "zt": (192, i32), "mm": (192, f32),
    "ww": (192, f32), "x2": (64, f32), "d": (32, b16), "ylu": (32, u16),
    "st": (96 * 7, f32), "u": (96 * 6, f32), "l3": (96, u16), "l12": (192, u16),
}
SCRATCH = {n: ("sbuf", [128, c], d) for n, (c, d) in _SB.items()}
for _b in range(8):
    SCRATCH["B%d" % _b] = ("psum", [128, 512], f32)
SEMAPHORES = ["cV", "cS", "cP", "cG", "ldx", "ldt", "ldr", "ldf", "arr0", "arr1", "arr2", "sent", "out"]


def rank_program(g, core, T, topo):
    rank = T.rank_of(core)
    if rank is None:
        return
    eng = {"V": g.vector, "S": g.scalar, "P": g.tensor, "G": g, "Y": g.sync}
    cnt = {}
    known = {e: {} for e in eng}
    clock = {}
    acc = {}

    def wait(e, sem, n):
        if known[e].get(sem, 0) >= n:
            return
        eng[e].wait_ge(T.sem[sem], n)
        known[e][sem] = n
        for s, m in clock.get((sem, n), {}).items():
            if known[e].get(s, 0) < m:
                known[e][s] = m

    def step(e, call, rd, wr, sem=None, inc=1):
        sem = sem or "c" + e
        need = {}
        for lst, isw in ((rd, False), (wr, True)):
            for (n, lo, hi) in lst:
                ps = SCRATCH[n][0] == "psum"
                for (l2, h2, w2, e2, s2, c2) in acc.get(n, []):
                    over = l2 < hi and lo < h2
                    if e2 == e and e == "P":
                        continue
                    if (over and (isw or w2)) or (ps and e2 != e):
                        if s2 == sem and inc == 16:
                            continue
                        need[s2] = max(need.get(s2, 0), cnt[s2] if s2[0] != "c" else c2)
        for s, n in need.items():
            wait(e, s, n)
        ins = call()
        cnt[sem] = cnt.get(sem, 0) + inc
        ins.then_inc(T.sem[sem], inc)
        clock[(sem, cnt[sem])] = dict(known[e])
        for lst, isw in ((rd, False), (wr, True)):
            for (n, lo, hi) in lst:
                old = acc.setdefault(n, [])
                if isw:
                    old[:] = [x for x in old if not (lo <= x[0] and x[1] <= hi)]
                old.append((lo, hi, isw, e, sem, cnt[sem]))

    def ap(x):
        a = T[x[0]][:, x[1]:x[2]]
        return a.indirect(T[x[3][0]][:, x[3][1]:x[3][2]]) if len(x) > 3 else a

    def keys(*xs):
        k = []
        for x in xs:
            if isinstance(x, tuple):
                k.append(x[:3])
                if len(x) > 3:
                    k.append(x[3])
        return k

    def val(x):
        return ap(x) if isinstance(x, tuple) else x

    def cp(o, a):
        step("V", lambda: g.vector.tensor_copy(ap(o), ap(a)), keys(a), keys(o))

    def tt(o, a, b, op):
        step("V", lambda: g.vector.tensor_tensor(ap(o), ap(a), ap(b), op), keys(a, b), keys(o))

    def ts(o, a, s1, o0, s2=None, o1=None):
        if o1 is None:
            step("V", lambda: g.vector.tensor_scalar(ap(o), ap(a), val(s1), None, o0), keys(a, s1), keys(o))
        else:
            step("V", lambda: g.vector.tensor_scalar(ap(o), ap(a), val(s1), val(s2), o0, o1), keys(a, s1, s2), keys(o))

    def fill(o, c):
        step("V", lambda: g.vector.memset(ap(o), c), [], keys(o))

    def act(o, a, scale=1.0, bias=None, func=None):
        if bias is None:
            step("S", lambda: g.scalar.activation(ap(o), ap(a), func or AF.Copy, scale=val(scale)), keys(a, scale), keys(o))
        else:
            step("S", lambda: g.scalar.activation(ap(o), ap(a), AF.Identity, bias=val(bias), scale=val(scale)), keys(a, scale, bias), keys(o))

    def iota(o, pat, base, cm):
        if _SB[o[0]][1] == i32:
            step("G", lambda: g.iota(ap(o), pat, base, cm), [], keys(o))
        else:
            step("G", lambda: g.iota(ap(o), pat, base, cm, allow_small_or_imprecise_dtypes=True), [], keys(o))

    def mm(group, rd, wr):
        def call():
            ins = None
            for (o, l, r, s, e) in group:
                ins = g.tensor.matmul(o, l, r, s, e)
            return ins
        step("P", call, rd, wr)

    def sums(terms, first=True, last=True):
        n = len(terms)
        mm([(ap(o), ap(l), ap(r), first and q == 0, last and q == n - 1) for q, (o, l, r) in enumerate(terms)],
           [x for t3 in terms for x in t3[1:]], [t3[0] for t3 in terms])

    def extract(out, z, src, first=True, last=True):
        o = ap(out)
        mm([(o, T.Z[:, 144 * z + 15 - i:144 * z + 143 - i], T[src[0]][:, src[1] + i:src[2]:16], first and i == 0, last and i == 15) for i in range(16)],
           [src, ("Z", 144 * z, 144 * z + 144)], [out])

    def spread(bank, L, src):
        mm([(T[bank][:, i:512:16], T[L][:, 128 * i:128 * i + 128], ap(src), True, True) for i in range(16)], [src, (L, 0, 2048)], [(bank, 0, 512)])

    def dma(e, o, a, rd, wr, sem):
        step(e, lambda: eng[e].dma_start(o, a), rd, wr, sem, 16)

    col = lambda n, j: (n, j, j + 1)
    blk = lambda n, j, w, o=0: (n, o + j * w, o + j * w + w)
    ZPAR, ZID, ZRES, ZNEXT, Z1, Z64, ZW2, ZP, ZB = 0, 1, 2, 5, 6, 7, 8, 9, 10
    SA, SP, SI, SB, I1, I2K, IP, IM, I512 = [blk("Sel", j, 128) for j in range(9)]
    IH, IHN = blk("Ih", 0, 128), blk("Ih", 1, 128)
    PF, CI, CG, TG, CH, C96, PM2, P8, PA, LT10, C512, CAB, CBI, EP, EM = [col("cf", j) for j in range(15)]
    c128, c144, zb = ("cols", 0, 128), ("cols", 0, 144), blk("Z", Z1, 144)
    fo = lambda t: 0 if t % 2 == 0 else 5632
    wo = lambda t: 0 if t % 2 == 0 else NB

    dma("Y", T.Xi[:, 0:96], T.par[:], [], [("Xi", 0, 96)], "ldx")
    for t in range(RO):
        dma("S" if t == 0 else "Y", T.Xi[:, 96 + 96 * t:192 + 96 * t], T.res[:, NB * t:NB * t + NB], [], [("Xi", 96 + 96 * t, 192 + 96 * t)], "ldx")
    dma("S", T.tiei[:], T.tie[:], [], [("tiei", 0, 192)], "ldt")
    iota(col("pi", 0), [[0, 1]], 0, 1)
    iota(c144, [[1, 144]], 0, 0)
    iota(("vl", 0, 96), [[16, 96]], 0, 1)
    iota(("wt", 0, 192), [[1, 3], [-4, 2], [0, 32]], 5, 0)
    iota(("W", NB, 2048), [[0, 512]], 0, 0)
    iota(("W", 7168, 7176), [[0, 8]], 0, 0)
    iota(("W", 3584, 4096), [[0, 512]], 0, 0)
    iota(("PW", 3584, 4096), [[0, 512]], 0, 0)
    iota(("iov", 0, NB), [[1, NB]], 0, 0)
    fill(("PW", 0, NB), 0.0)
    ts(col("pi", 1), col("pi", 0), 15, A.bitwise_and)
    cp(PF, col("pi", 0))
    cp(CI, col("pi", 1))
    ts(col("pi", 2), col("pi", 1), 1, A.arith_shift_right)
    ts(C96, col("pi", 1), 96.0, A.mult)
    tt(CG, PF, CI, A.subtract)
    cp(CH, col("pi", 2))
    ts(("Xi", 384, 480), ("cols", 0, 96), C96, A.add)
    ts(TG, CG, 15.0, A.add)
    ts(("ev", 0, 16), ("cols", 0, 16), CI, A.is_equal)
    ts(("bb", 0, 128), c128, CG, A.is_ge)
    ts(("bb", 128, 256), c128, TG, A.is_le)
    cp(("XH", 0, 480), ("Xi", 0, 480))
    rows = ((0, 0), (1, 4), (4, 2), (2, 6), (3, 8))
    for b, r in rows:
        dma("Y", T.PW[r:128:16, 0:NB], T.XH[:, 96 * b:96 * b + 96], [("XH", 0, 480)], [("PW", 0, NB)], "ldr")
    tt(("XL", 0, 480), ("Xi", 0, 480), ("XH", 0, 480), A.subtract)
    for b, r in rows:
        dma("S", T.PW[r + 1:128:16, 0:NB], T.XL[:, 96 * b:96 * b + 96], [("XL", 0, 480)], [("PW", 0, NB)], "ldr")
    wait("Y", "ldr", cnt["ldr"])
    dma("Y", T.W[:, 0:NB], T.fl[:], [], [("W", 0, NB)], "ldf")
    tt(("bb", 256, 384), ("bb", 0, 128), ("bb", 128, 256), A.mult)
    ts(("hv", 0, 8), ("cols", 0, 8), CH, A.is_equal)
    ts(zb, c144, TG, A.is_equal)
    ts(("ev", 16, 32), ("ev", 0, 16), 2048.0, A.mult)
    cp(("tieu", 0, 192), ("tiei", 0, 192))
    for c in (0, 2):
        act(blk("Z", c, 144), zb, col("hv", c))
    for i in range(11):
        act(blk("Lf", i, 128), ("bb", 256, 384), col("ev", i))
    ts(IH, c128, PF, A.is_equal)
    ts(IHN, c128, PF, A.is_equal, -1.0, A.mult)
    ts(I2K, c128, PF, A.is_equal, 2048.0, A.mult)
    ts(I1, c128, PF, A.is_equal)
    ts(("vl", 0, 96), ("vl", 0, 96), CG, A.subtract)
    cp(("Ch", 0, 64), ("tiei", 0, 64))
    cp(("zh", 0, 32), ("vl", 0, 32))
    cp(("zh", 32, 64), ("vl", 0, 32))
    fill(("ones", 0, 32), 1.0)
    fill(EP, EPS)
    fill(EM, -EPS)
    ts(PM2, PF, -2.0, A.add)
    ts(P8, PF, 8.0, A.add)
    ts(PA, col("hv", 0), 10.0, A.mult, PF, A.add)
    ts(LT10, CI, 10.0, A.is_lt)
    ts(C512, CI, 512.0, A.mult)
    ts(CAB, CI, 4.0, A.is_ge, 1.0, A.add)
    gapV, gapS = [], []
    for i in range(11, 16):
        gapS.append(lambda i=i: act(blk("Lf", i, 128), ("bb", 256, 384), col("ev", i)))
    for i in range(16):
        gapS.append(lambda i=i: act(blk("Lb", i, 128), ("bb", 256, 384), col("ev", 16 + i)))
        gapV.append(lambda i=i: ts(blk("Zi", i, 144), zb, col("ev", i), A.mult))

    def late_v(part):
        if part == 0:
            ts(col("pi", 3), col("pi", 0), 3, A.bitwise_and)
            ts(col("bb", 0), CI, 8.0, A.is_ge)
            fill(("mm", 0, 192), 132.0)
            ts(col("bb", 1), col("pi", 3), 0.0, A.is_equal, col("bb", 0), A.max)
            ts(CBI, col("bb", 1), -5.0, A.mult)
        else:
            for s, tg, w in ((SA, PA, LT10), (SP, PM2, col("hv", 1)), (SI, PF, col("hv", 1)), (SB, P8, col("hv", 1))):
                ts(s, c128, tg, A.is_equal, w, A.mult)

    def late_s():
        for z, w in ((Z64, float(W1)), (ZW2, float(W2)), (ZP, C512), (ZB, CAB), (1, col("hv", 1)), (3, col("hv", 3)),
                     (4, col("hv", 4)), (5, col("hv", 5))):
            act(blk("Z", z, 144), zb, w)
        for s, w in ((IP, 99.0), (IM, -99.0), (I512, 512.0)):
            act(s, I1, w)
        for q in range(2):
            act(blk("zv", q, 96), ("vl", 0, 96), 1.0, float(fo(q) - wo(q)))

    def gap(lst, n):
        for f in lst[:n]:
            f()
        del lst[:n]

    peers = [c for c in T.cores if c != core]
    near = [c for c in peers if c in topo.cores_of(core)]
    far = [c for c in peers if c not in near]
    fe = topo.engines(core, far[0])
    masks = {}
    for j, c in enumerate(far):
        masks[c] = fe[j * len(fe) // len(far):(j + 1) * len(fe) // len(far)]
    for c in near:
        masks[c] = [e for e in topo.engines(core, c) if e not in fe]
    arrivals = sum(len(m) for m in masks.values())

    ONL, ZD, LO, HI, ISB, RR, OWN = [blk("st", j, 96) for j in range(7)]
    T2, KK, PH, PD, L1F, L2F = [blk("u", j, 96) for j in range(6)]
    EE, PA1, TU, PA2, YY = [blk("B5", j, 96) for j in range(5)]
    RES = ("B0", 256, 352)

    def update_base(t, a, b):
        act(("base", 16 * a, 16 * b), ("W", wo(t), wo(t) + 5632, ("l12", 96 + a, 96 + b)))

    def update(t, a, b):
        tt(("W", fo(t + 1) + 16 * a, fo(t + 1) + 16 * b), ("W", wo(t), wo(t) + 5632, ("l12", a, b)), ("base", 16 * a, 16 * b), A.subtract)

    def lists12(part):
        if part == 0:
            ts(PA1, TU, 512.0, A.mult)
            tt(PH, TU, ISB, A.not_equal)
            tt(YY, OWN, PA1, A.subtract)
            tt(PA2, KK, YY, A.subtract)
        else:
            tt(PD, PA2, PH, A.mult)
            tt(L1F, YY, PD, A.add)
            tt(L2F, KK, PD, A.subtract)
            cp(("l12", 0, 192), ("u", 96 * 4, 96 * 6))

    def list3(t):
        tt(PA2, TU, RR, A.mult)
        tt(PA1, PA2, blk("zv", t % 2, 96), A.add)
        cp(("l3", 0, 96), PA1)

    def table_v(t, n):
        cp(("PW", fo(t + 1), fo(t + 1) + 16 * n), ("PW", wo(t), wo(t) + 5632, ("l3", 0, n)))

    def table_s(t, n):
        act(("PW", fo(t + 1) + 16 * n, fo(t + 1) + NB), ("PW", wo(t), wo(t) + 5632, ("l3", n, 96)))

    def ends_gather(t):
        act(("ytg", 0, NT), ("PW", wo(t), wo(t) + 5632, ("ylu", 0, 32)))

    def ends_lists(t):
        extract(("B6", 0, 32), ZID, ("ytg", 0, NT))
        extract(("B6", 32, 64), ZNEXT, ("ytg", 0, NT))
        act(("yts", 64 * t, 64 * t + 64), ("B6", 0, 64))

    def res_use(t, src):
        cp(blk("ru", t, 96), src)
        ts(blk("zc", t, 96), src, float(NB - wo(t)), A.add)

    def diffs(lo, hi):
        grp = []
        for n in range(lo, hi):
            i, j = PAIRS[n]
            o = T.B3[:, 32 * n:32 * n + 32]
            grp += [(o, ap(IH), T.Ch[:, 64 * i:64 * i + 32], True, False), (o, ap(IHN), T.Ch[:, 64 * j + 32:64 * j + 64], False, True)]
        mm(grp, [("Ch", 0, 64 * (max(PAIRS[hi - 1]) + 1)), ("Ih", 0, 256)], [("B3", 32 * lo, 32 * hi)])

    def eq(lo, hi):
        ts(("E", 32 * lo, 32 * hi), ("B3", 32 * lo, 32 * hi), 0.0, A.is_equal)

    def met(lo, hi):
        r = []
        for n in range(lo, hi):
            i, j = PAIRS[n]
            r += [(blk("B2", 2 * k, 32), I2K, blk("E", n, 32)) for k in range(i, 3)]
            r += [(blk("B2", 2 * k + 1, 32), I2K, blk("E", n, 32)) for k in range(j, 3)]
        return r

    def res_diff(t, k):
        extract(blk("B1", k, 64), ZRES + t, blk("O", k, 1024), True, False)
        sums([(blk("B1", k, 64), IHN, ("zh", 0, 64))], False, True)

    Ok = lambda k, s: blk("O", 2 * k + s, 512)
    plan = [(CODE[k][s], SA, Ok(k, s), SP, Ok(k - 1, s) if k else Ok(0, 1 - s)) for k in range(3) for s in range(2)]
    plan.append((0, SI, Ok(0, 0), SB, Ok(0, 1)))

    def blocks(lo, hi):
        for n in range(lo, hi):
            c, s1, r1, s2, r2 = plan[n]
            bank = (("B7", "B6")[n % 2], 0, 512)
            sums([(bank, s1, r1), (bank, s2, r2)])
            act(blk("PW", c, 512, NB), bank)

    extract(("B7", 128, 224), ZRES, ("PW", 0, NB))
    for t in range(RO):
        tab = ("PW", fo(t), fo(t) + NB)
        for k in range(3):
            ls, lo = ("tieu", 64 * t) if k == 0 else ("Cu", 64 * (k - 1))
            cp(Ok(k, 0), tab + ((ls, lo, lo + 32),))
            act(Ok(k, 1), tab + ((ls, lo + 32, lo + 64),))
            Cn = blk("B0", k, 64)
            extract(Cn, ZPAR, blk("O", k, 1024))
            if k == 1:
                eq(0, 4)
            if k == 2:
                eq(4, 9)
                sums(met(4, 9), False, False)
            if t > 0:
                if k < 2:
                    lists12(k)
                if k > 0:
                    update_base(t - 1, 32 * k - 32, 32 * k)
                if k == 2:
                    update_base(t - 1, 64, 96)
                    update(t - 1, 0, 32)
            else:
                gap(gapV, 5)
                gap(gapS, 4)
            if k < 2:
                cp(blk("Cu", k, 64), Cn)
            cp(blk("Ch", k + 1, 64), Cn)
            diffs(*((0, 4), (4, 9), (9, 16))[k])
            if k == 0:
                res_diff(t, 0)
            if k == 1:
                sums([(("B2", 0, 192), IH, ("Ch", 0, 192))] + met(0, 4), True, False)
        if t > 0:
            update(t - 1, 32, 64)
        else:
            gap(gapV, 1)
            res_use(0, ("B7", 128, 224))
            gap(gapS, 9)
        eq(9, 16)
        sums(met(9, 15), False, True)
        if t > 0:
            update(t - 1, 64, 96)
        else:
            late_v(0)
        ts(("SLu", 0, 192), ("B2", 0, 192), float(NB), A.min)
        fw = ("W", fo(t), fo(t) + NB + 8)
        G = lambda k, s: blk("W", CODE[k][s], 512, NB)
        slot = lambda k, s: fw + (blk("SLu", 2 * k + s, 32),)
        for k, s in ((0, 1), (1, 0), (1, 1), (2, 0), (2, 1)):
            act(G(k, s), slot(k, s), -1.0 if s else 1.0)
        ts(("SLh", 0, 192), ("B2", 0, 192), float(NB), A.min)
        ts(("on", 0, 192), ("SLh", 0, 192), float(NB), A.is_lt)
        cp(G(0, 0), slot(0, 0))
        sums([(("B2", 192, 224), I1, blk("on", s, 32)) for s in range(6)] + [(("B2", 192, 224), I1, ("ones", 0, 32))])
        sums([(("B2", 224, 256), I1, blk("E", n, 32)) for n in range(16)])
        res_diff(t, 1)
        step("V", lambda: g.vector.reciprocal(T.rn[:], T.B2[:, 192:224]), [("B2", 192, 224)], [("rn", 0, 32)])
        ts(("nf", 0, 32), ("B2", 224, 256), 0.0, A.is_equal)
        spread("B5", "Lf", ("rn", 0, 32))
        res_diff(t, 2)
        grp = []
        for i in range(16):
            for s in range(6):
                c = CODE[s // 2][s % 2]
                grp.append((T.B6[:, i:512:16], T.Zi[:, 144 * i + 15 - c:144 * i + 143 - c], ap(blk("SLh", s, 32)), s == 0, False))
            grp.append((T.B6[:, i:512:16], T.Lb[:, 128 * i:128 * i + 128], T.nf[:], False, True))
        mm(grp, [("Zi", 0, 2304), ("SLh", 0, 192), ("Lb", 0, 2048), ("nf", 0, 32)], [("B6", 0, 512)])
        ac = ("B4", 0, 512)
        tt(ac, G(0, 0), G(0, 1), A.add)
        tt(ac, ac, G(1, 0), A.add)
        tt(ac, ac, G(1, 1), A.add)
        tt(ac, ac, G(2, 0), A.add)
        tt(("Dsb", 0, NT), ac, G(2, 1), A.add)
        tt(("Dp", 0, NT), ("Dsb", 0, NT), ("B5", 0, 512), A.mult)
        act(("B4", 0, 512), ("Dp", 0, NT), 1.0, EP)
        act(("B5", 0, 512), ("Dp", 0, NT), 1.0, EM)
        tt(("m", 0, 192), ("B1", 0, 192), ("on", 0, 192), A.mult)
        act(("mis", 0, 192), ("m", 0, 192), 1.0, None, AF.Abs)
        if t == 0:
            late_v(1)
            late_s()
        else:
            res_use(t, RES)
            ends_gather(t - 1)
        act(("slotw", 0, NT), ("B6", 0, 512), 1.0, CBI)
        if t < RO - 1:
            cp(("Ch", 0, 64), ("tiei", 64 * t + 64, 64 * t + 128))
        for k in range(3):
            tt(blk("votes", 2 * k, 512), G(k, 0), ("B4", 0, 512), A.is_le)
            tt(blk("votes", 2 * k + 1, 512), G(k, 1), ("B5", 0, 512), A.is_ge)
            extract(("B2", 256, 320), (Z1, Z64, ZW2)[k], blk("votes", k, 1024), k == 0, k == 2)
            if k < 2:
                blocks(k, k + 1)
        snd = blk("snd", t, 64)
        cp(snd, ("B2", 256, 320))
        wait("G", "cV", cnt["cV"])
        trs = []
        for c in peers:
            rid, pid = topo.addr(c, core)
            j = [x for x in T.cores if x != c].index(core)
            trs.append(RemoteDMATransfer(dst_ids=[DstId(rid=rid, pnc=pid)], dma_engine_mask=sum(1 << e for e in masks[c]), remote_sem=T.sem["arr%d" % t],
                                         src=ap(snd), dst=T.land[:, 192 * t + 64 * j:192 * t + 64 * j + 64]))
        g.remote_dma_fused(trs, local_sem=T.sem.sent)
        ohk = ("oh", 0, NB)
        tt(ohk, ("slotw", 0, NT, blk("ru", t, 96)), ("iov", 0, NB), A.is_equal)
        sums([(("B1", 192, 224), I1, blk("mis", s, 32)) for s in range(6)] + [(("B1", 192, 224), I1, ("nf", 0, 32))])
        act(("mis", 0, 32), ("B1", 192, 224))
        sums([(("B3", 0, 192), IP, ("on", 0, 192))], True, False)
        for k in range(3):
            extract(blk("B3", k, 64), Z1, blk("votes", k, 1024), False, False)
        sums([(blk("B3", b, 32), IM, ("mis", 0, 32)) for b in range(6)], False, True)
        blocks(2, 4)
        tt(ZD, blk("zc", t, 96), blk("zv", t % 2, 96), A.subtract)
        extract(blk("B1", 0, 96), ZP, ohk)
        extract(blk("B1", 1, 96), ZB, ohk)
        act(ONL, blk("B1", 0, 96), 1.0, None, AF.Sign)
        act(LO, blk("B1", 0, 96))
        act(HI, blk("B1", 1, 96), 2048.0, -512.0)
        blocks(4, 6)
        wait("V", "arr%d" % t, arrivals)
        step("V", lambda: g.vector.tensor_copy(T.lf[:], T.land[:, 192 * t:192 * t + 192]), [], [("lf", 0, 192)])
        tt(("s1", 0, 64), ("lf", 0, 64), ("lf", 64, 128), A.add)
        tt(("S", 0, 64), ("s1", 0, 64), ("lf", 128, 192), A.add)
        ts(("zt", 128, 192), ("S", 0, 64), 1.0 / W2, A.mult, -0.393, A.add)
        ts(("zt", 0, 64), ("S", 0, 64), W1 - 1, A.bitwise_and)
        ts(("zt", 64, 128), ("S", 0, 64), 6, A.arith_shift_right)
        ts(("mm", 64, 128), ("zt", 128, 192), float(W2 // W1), A.mult, 132.0, A.add)
        tt(("B3", 192, 384), ("B3", 0, 192), ("zt", 0, 192), A.add)
        tt(("B3", 0, 192), ("B3", 192, 384), ("mm", 0, 192), A.is_ge)
        tt(("ww", 0, 192), ("B3", 0, 192), ("wt", 0, 192), A.mult)
        tt(("B3", 384, 448), ("ww", 0, 64), ("ww", 64, 128), A.max)
        tt(("x2", 0, 64), ("B3", 384, 448), ("ww", 128, 192), A.max)
        tt(("d", 0, 32), ("x2", 0, 32), ("x2", 32, 64), A.max)
        spread("B4", "Lb", ("d", 0, 32))
        act(("dwin", 0, NT), ("B4", 0, 512), 0.5 / 4)
        sums([(("B0", 192, 224), I512, ("d", 0, 32)), (("B0", 192, 224), IH, ("zh", 0, 32))])
        tt(blk("B1", 2, 96), blk("B1", 0, 96), ZD, A.add)
        ts(ISB, blk("B1", 1, 96), 1.0, A.is_equal)
        tt(RR, blk("B1", 2, 96), ONL, A.mult)
        tt(OWN, RR, blk("zv", t % 2, 96), A.add)
        ts(("ylu", 0, 32), ("B0", 192, 224), float(NB - wo(t)), A.add)
        cp(("eg", 0, 768), ("dwin", 0, NT, ("ru", 96 * t, 96 * t + 48)))
        act(("eg", 768, NB), ("dwin", 0, NT, ("ru", 96 * t + 48, 96 * t + 96)))
        blocks(6, 7)
        if t > 0:
            ends_lists(t - 1)
        extract(EE, ZPAR, ("eg", 0, NB))
        if t < RO - 1:
            extract(RES, ZRES + t + 1, tab)
        else:
            ends_gather(t)
        tt(PA1, EE, LO, A.is_ge)
        tt(T2, EE, HI, A.is_le)
        tt(PA2, EE, ONL, A.mult)
        tt(TU, PA1, T2, A.mult)
        tt(KK, PA2, blk("zc", t, 96), A.add)
        list3(t)
        if t < RO - 1:
            table_v(t, TS)
            table_s(t, TS)
        else:
            o = fo(t + 1)
            table_s(t, TL)
            ends_lists(t)
            dma("Y", T.yt[:], T.yts[:], [("yts", 0, 192)], [], "out")
            lists12(0)
            lists12(1)
            cuts = (0, 32, 64, 80, 96)
            for a, b in zip(cuts, cuts[1:]):
                update_base(t, a, b)
            table_v(t, TL)
            for a, b in zip(cuts, cuts[1:]):
                update(t, a, b)
                dma("Y", T.yf[:, 16 * a:16 * b], T.W[:, o + 16 * a:o + 16 * b], [("W", o + 16 * a, o + 16 * b)], [], "out")
            for c in range(3):
                bank = ("B4", "B6", "B3")[c]
                src = blk("PW", c, 512, o)
                mm([(T[bank][0:8, :], T.Z[:, 15:143:16], ap(src), True, True)], [src, blk("Z", ZPAR, 144)], [(bank, 0, 512)])
                if c == 2:
                    step("V", lambda: g.vector.tensor_copy(T.yps[0:8, 512 * c:512 * c + 512], T[bank][0:8, :]), [(bank, 0, 512)], [blk("yps", c, 512)])
                else:
                    step("S", lambda: g.scalar.activation(T.yps[0:8, 512 * c:512 * c + 512], T[bank][0:8, :], AF.Copy), [(bank, 0, 512)], [blk("yps", c, 512)])
            dma("S", T.yp[:], T.yps[0:8, :], [("yps", 0, NB)], [], "out")
    for s in ("cV", "cS", "cP", "cG", "ldx", "ldt", "ldr", "ldf", "out"):
        g.wait_ge(T.sem[s], cnt[s])
    g.wait_ge(T.sem.sent, RO * arrivals)
